import numpy as np
import ml_dtypes


def mxq(x, axis, fmt="e4m3"):
    dtype, down = {"e4m3": (ml_dtypes.float8_e4m3fn, 7), "e5m2": (ml_dtypes.float8_e5m2, 14)}[fmt]
    v = np.moveaxis(np.asarray(x, np.float32).astype(ml_dtypes.bfloat16).astype(np.float64), axis, -1)
    blocks = v.reshape(v.shape[:-1] + (-1, 32))
    amax = np.abs(blocks).max(-1, keepdims=True)
    byte = np.maximum(np.where(amax > 0, np.frexp(amax)[1] - 1 + 127, 0) - down, 1)
    scale = np.exp2(byte - 127.0)
    codes = (blocks / scale).astype(np.float32).astype(dtype).astype(np.float64)
    return np.moveaxis((codes * scale).reshape(v.shape), -1, axis)


WIDE = False


def mx_kscale(k):
    if not WIDE:
        return np.ones(k)
    levels = np.array([10, -10, 5, -5, 0])
    if k % 512:
        return np.exp2(np.random.permutation(np.resize(levels, k // 32))).repeat(32)
    a = np.empty((k // 512, 16))
    for p in range(k // 512):
        a[p, :8] = np.random.permutation(np.resize(levels, 8))
        for g in range(8):
            far = levels[np.abs(levels - a[p, g]) >= 10]
            a[p, g + 8] = far[np.random.randint(len(far))]
    return np.exp2(a.ravel()).repeat(32)


def f64(x):
    return np.asarray(x).astype(np.float64)


def striped(idx):
    return np.tile(idx.reshape(-1, 16).T, (8, 1)).astype(np.uint16)


def unstriped(offs):
    return offs[:16].T.reshape(-1).astype(np.int64)


E2M1 = np.array([0.0, 0.5, 1.0, 1.5, 2.0, 3.0, 4.0, 6.0, -0.0, -0.5, -1.0, -1.5, -2.0, -3.0, -4.0, -6.0])


def pack_weight(w, fmt):
    k, n = w.shape
    w = f64(np.asarray(w, np.float32).astype(ml_dtypes.bfloat16)).reshape(k // 32, 32, n)
    amax = np.abs(w).max(1)
    if fmt == "e4m3":
        byte = np.frexp(amax)[1] - 1 + 127 - 7
    else:
        mant, ex = np.frexp(amax / 6.0)
        byte = np.where(mant > 0.5, ex, ex - 1) + 127
    byte = np.clip(np.where(amax > 0, byte, 1), 1, 254)
    scaled = (w * np.exp2(127.0 - byte)[:, None, :]).reshape(k, n).astype(np.float32)
    by_word = np.ascontiguousarray(scaled.reshape(k // 512, 128, 4, n).transpose(0, 1, 3, 2))
    if fmt == "e4m3":
        words = by_word.astype(ml_dtypes.float8_e4m3fn).view(np.uint8)
    else:
        c = by_word.astype(ml_dtypes.float4_e2m1fn).view(np.uint8) & 0xF
        words = (c[..., 0::2] | (c[..., 1::2] << 4)).reshape(k // 512, 128, 2 * n)
    return np.ascontiguousarray(words), np.ascontiguousarray(byte.astype(np.uint8).reshape(k // 512, 16, n))


def unpack_weight(words, scales, fmt):
    g, _, n = scales.shape
    words = np.ascontiguousarray(words).reshape(g, 128, n, -1)
    if fmt == "e4m3":
        vals = words.view(ml_dtypes.float8_e4m3fn).astype(np.float64)
    else:
        nib = np.empty((g, 128, n, 4), np.uint8)
        nib[..., 0::2] = words & 0xF
        nib[..., 1::2] = words >> 4
        vals = E2M1[nib]
    vals = vals * np.repeat(np.exp2(scales.astype(np.float64) - 127.0), 8, axis=1)[..., None]
    return vals.transpose(0, 1, 3, 2).reshape(g * 512, n)


def gelu(v):
    return 0.5 * v * (1.0 + np.tanh(np.sqrt(2.0 / np.pi) * (v + 0.044715 * v**3)))


def bf(x):
    return np.asarray(x, np.float32).astype(ml_dtypes.bfloat16)


def planes(Y):
    n, m = Y.shape
    b = f64(bf(Y)).reshape(n // 32, 32, m)
    amax = np.abs(b).max(1)
    byte = np.clip(np.where(amax > 0, np.frexp(amax)[1] - 1 + 127 - 7, 1), 1, 254)
    codes = (b * np.exp2(127.0 - byte)[:, None, :]).reshape(n, m).astype(np.float32).astype(ml_dtypes.float8_e4m3fn).view(np.uint8)
    words = codes.reshape(n // 512, 128, 4, m).transpose(0, 1, 3, 2)
    return np.ascontiguousarray(words), np.ascontiguousarray(byte.astype(np.uint8).reshape(n // 512, 16, m))


K, T, S, H, N, P = 1536, 4096, 1024, 512, 1024, 512

def setup_inputs():
    n = np.random.standard_normal
    s = mx_kscale(K)[:, None]
    u = mx_kscale(H)[:, None]
    tab_words, tab_scales = pack_weight(n((K, T)) * s, "e4m3")
    w2_words, w2_scales = pack_weight(1.3 * n((H, N)) / np.sqrt(H) / u, "e2m1")
    g = np.exp(0.8 * n(N))
    signs = np.where(n(N) > 0, 1.0, -1.0)
    return {
        "tab_words": tab_words, "tab_scales": tab_scales,
        "offs": striped(np.random.permutation(T)[:S]),
        "pos1": striped(np.random.permutation(S)[:P]),
        "pos2": striped(np.random.permutation(S)[:P]),
        "w1": (n((K, H)) / np.sqrt(K) / s * u.T).astype(np.float32),
        "lim": ((0.5 + 0.8 * n((H, S))) * u).astype(np.float32),
        "w2_words": w2_words, "w2_scales": w2_scales,
        "w3": (0.5 * n((H, N)) / np.sqrt(H) / u).astype(np.float32),
        "slope": np.random.uniform(1, 3, N).astype(np.float32),
        "share": np.random.uniform(0.1, 0.5, N).astype(np.float32),
        "sgn": (signs * np.random.uniform(1.5, 3.0, N) * g).astype(np.float32),
        "base": (0.6 * n((N, P)) * g[:, None]).astype(np.float32),
        "gain": g.astype(np.float32),
    }

def reference(tab_words, tab_scales, offs, pos1, pos2, w1, lim, w2_words, w2_scales, w3, slope, share, sgn, base, gain):
    v = unpack_weight(tab_words, tab_scales, "e4m3")[:, unstriped(offs)]
    h = np.minimum(mxq(f64(w1), 0, "e4m3").T @ v, f64(lim))
    hq = mxq(h, 0, "e4m3")
    w2 = unpack_weight(w2_words, w2_scales, "e2m1")
    e = np.tanh(w2.T @ hq) + (mxq(f64(w3), 0, "e4m3").T @ hq)
    top = e.max(axis=1)
    look = 1.0 / (1.0 + np.exp(-f64(slope)[:, None] * (e[:, unstriped(pos1)] - f64(share)[:, None] * top[:, None])))
    a = look * f64(sgn)[:, None] + f64(base)
    c = f64(gain)[:, None] * e[:, unstriped(pos2)]
    y = np.minimum(a, c)
    words, scales = planes(y)
    return y, words, scales

@@ -1,0 +1,336 @@
+from contextlib import ExitStack
+
+import concourse.mybir as mybir
+from concourse.masks import make_identity
+
+K, T, S, H, N, M = 1536, 4096, 1024, 512, 1024, 512
+FLOPS = 2 * K * H * S + 2 * 2 * H * N * S
+
+F32 = mybir.dt.float32
+BF16 = mybir.dt.bfloat16
+I32 = mybir.dt.int32
+U32 = mybir.dt.uint32
+U16 = mybir.dt.uint16
+U8 = mybir.dt.uint8
+FP8X4 = mybir.dt.float8_e4m3fn_x4
+FP4X4 = mybir.dt.float4_e2m1fn_x4
+ALU = mybir.AluOpType
+ACT = mybir.ActivationFunctionType
+
+P = 128
+PASSES = K // 512
+CHUNKS = S // P
+PAIRS = CHUNKS // 2
+GROUPS = N // 512
+
+
+def tile_list_pallet_shortage_scores_kernel(
+    tc, tab_words, tab_scales, offs, pos1, pos2, w1, lim, w2_words, w2_scales, w3,
+    slope, share, sgn, base, gain, out_0, out_1, out_2,
+):
+    nc = tc.nc
+    with ExitStack() as ctx:
+        keep = ctx.enter_context(tc.tile_pool(name="keep", bufs=1))
+        ring = ctx.enter_context(tc.tile_pool(name="ring", bufs=2))
+        psum = ctx.enter_context(tc.psum_pool(name="psum", bufs=4))
+
+        offs_t = keep.tile([P, S // 16], U16, name="offs_t")
+        pos1_t = keep.tile([P, M // 16], U16, name="pos1_t")
+        pos2_t = keep.tile([P, M // 16], U16, name="pos2_t")
+        tab_s = keep.tile([P, T], U8, name="tab_s", align_bytes=64)
+        w2_raw = keep.tile([P, 2 * N], U8, name="w2_raw", align_bytes=64)
+        w2s_raw = keep.tile([P, N], U8, name="w2s_raw", align_bytes=64)
+        w2_q = keep.tile([P, 2 * N], U8, name="w2_q", align_bytes=64)
+        w2_s = keep.tile([P, N], U8, name="w2_s", align_bytes=64)
+        v_s = keep.tile([P, S], U8, name="v_s", align_bytes=64)
+        ident = keep.tile([P, P], F32, name="ident", align_bytes=64)
+        make_identity(nc, ident[:])
+        nc.vector.memset(tab_s[:].bitcast(I32), 0)
+        nc.vector.memset(w2s_raw[:].bitcast(I32), 0)
+
+        def load_tab(a):
+            t = ring.tile([P, T], I32, name="tab%d" % a, tag="big", bufs=4, align_bytes=64)
+            nc.sync.dma_start(out=t[:], in_=tab_words[a].rearrange("p t i -> p (t i)").bitcast(I32))
+            return t
+
+        def load_rows(src, name, tag, bufs):
+            t = ring.tile([P, 4, src.shape[1]], F32, name=name, tag=tag, bufs=bufs, align_bytes=64)
+            nc.sync.dma_start(out=t[:], in_=src.rearrange("(p j) c -> p j c", j=4))
+            return t
+
+        def load_vec(src, name):
+            t = keep.tile([P, 4 * GROUPS], F32, name=name)
+            nc.gpsimd.dma_start(
+                out=t[:].rearrange("p (g t) -> p g t", t=4),
+                in_=src.rearrange("(g p t) -> p g t", p=P, t=4),
+            )
+            return t
+
+        tab, w1_raw = [], []
+        tab.append(load_tab(0))
+        nc.sync.dma_start(offs_t[:], offs)
+        w1_raw.append(load_rows(w1[0:512, :], "w1r0", "raw", 3))
+        nc.sync.dma_start(out=w2_raw[:].bitcast(I32), in_=w2_words[0].bitcast(I32))
+        for q in range(4):
+            nc.sync.dma_start(
+                out=tab_s[32 * q : 32 * q + 4 * PASSES, :].bitcast(I32),
+                in_=tab_scales[:, 4 * q : 4 * q + 4, :].bitcast(I32),
+            )
+        tab.append(load_tab(1))
+        for q in range(4):
+            nc.gpsimd.dma_start(
+                out=w2s_raw[32 * q : 32 * q + 4, :].bitcast(I32),
+                in_=w2_scales[0, 4 * q : 4 * q + 4, :].bitcast(I32),
+            )
+        w1_raw.append(load_rows(w1[512:1024, :], "w1r1", "raw", 3))
+        tab.append(load_tab(2))
+        w1_raw.append(load_rows(w1[1024:1536, :], "w1r2", "raw", 3))
+        lim_t = [load_rows(lim[:, 0:512], "lim0", "lim0", 1)]
+        w3_raw = [load_rows(w3[:, 0:512], "w3r0", "w3r", 2)]
+        lim_t.append(load_rows(lim[:, 512:768], "lim1", "lim1", 1))
+        lim_t.append(load_rows(lim[:, 768:1024], "lim2", "lim2", 1))
+        w3_raw.append(load_rows(w3[:, 512:1024], "w3r1", "w3r", 2))
+        nc.sync.dma_start(pos1_t[:], pos1)
+        nc.sync.dma_start(pos2_t[:], pos2)
+        slope_t = load_vec(slope, "slope_t")
+        share_t = load_vec(share, "share_t")
+        sgn_t = load_vec(sgn, "sgn_t")
+        gain_t = load_vec(gain, "gain_t")
+        base_t = [load_rows(base[0:512, :], "base0", "base", 2)]
+        base_t.append(load_rows(base[512:1024, :], "base1", "base", 2))
+
+        def deal(copy, raw, staged, t0, t1):
+            copy(
+                out=staged[:].rearrange("p (t m j) -> p m j t", t=4, j=4)[:, :, :, t0:t1],
+                in_=raw[:].rearrange("p j (m t) -> p m j t", t=4)[:, :, :, t0:t1],
+            )
+
+        acc = [
+            psum.tile([P, 512], F32, name="acc%d" % c, tag="ab" if c < 4 else "e")
+            for c in range(CHUNKS)
+        ]
+        for a in range(PASSES):
+            v_w = keep.tile([P, S], U32, name="v_w%d" % a, align_bytes=64)
+            nc.vector.tensor_copy(v_w[:], tab[a][:].bitcast(U32).indirect(offs_t[:]))
+            if a == 0:
+                nc.vector.tensor_copy(v_s[:], tab_s[:].indirect(offs_t[:]))
+            staged = ring.tile([P, 2048], BF16, name="w1b%d" % a, tag="staged", bufs=3, align_bytes=64)
+            if a == PASSES - 1:
+                deal(nc.scalar.copy, w1_raw[a], staged, 0, 1)
+                deal(nc.vector.tensor_copy, w1_raw[a], staged, 1, 4)
+            else:
+                deal(nc.scalar.copy, w1_raw[a], staged, 0, 4)
+            w1_q = keep.tile([P, 512], U32, name="w1q%d" % a, align_bytes=64)
+            w1_s = keep.tile([P, 512], U8, name="w1s%d" % a, align_bytes=64)
+            nc.vector.quantize_mx(out=w1_q[:].bitcast(FP8X4), scales=w1_s[:], in_=staged[:])
+            if a == 0:
+                nc.vector.tensor_copy(
+                    out=w2_q[:].rearrange("p (g t m b) -> p g t m b", g=GROUPS, t=4, b=2),
+                    in_=w2_raw[:].rearrange("p (g m t b) -> p g t m b", g=GROUPS, t=4, b=2),
+                )
+                nc.vector.tensor_copy(
+                    out=w2_s[:].rearrange("p (g t m) -> p g t m", g=GROUPS, t=4),
+                    in_=w2s_raw[:].rearrange("p (g m t) -> p g t m", g=GROUPS, t=4),
+                )
+            for c in range(CHUNKS):
+                cols = slice(P * c, P * (c + 1))
+                for t in range(4):
+                    rows = slice(P * t, P * (t + 1))
+                    nc.tensor.matmul_mx(
+                        out=acc[c][:, rows],
+                        lhsT=w1_q[:, rows].bitcast(FP8X4),
+                        lhsT_scale=w1_s[:, rows],
+                        rhs=v_w[:, cols].bitcast(FP8X4),
+                        rhs_scale=v_s[4 * a : P, cols],
+                        start=(a == 0 and t == 0),
+                        stop=(a == PASSES - 1 and t == 3),
+                    )
+
+        h_q = [keep.tile([P, 256], U32, name="hq%d" % k, align_bytes=64) for k in range(PAIRS)]
+        h_s = [keep.tile([P, 256], U8, name="hs%d" % k, align_bytes=64) for k in range(PAIRS)]
+        h_b = [
+            ring.tile([P, 1024], BF16, name="hb%d" % k, tag="hb", bufs=4, align_bytes=64)
+            for k in range(PAIRS)
+        ]
+        w3_q = [keep.tile([P, 256], U32, name="w3q%d" % q, align_bytes=64) for q in range(4)]
+        w3_s = [keep.tile([P, 256], U8, name="w3s%d" % q, align_bytes=64) for q in range(4)]
+        parts = [
+            ring.tile([P, 4096], F32, name="parts%d" % q, tag="big", bufs=4, align_bytes=64)
+            for q in range(4)
+        ]
+
+        def cap(c):
+            piece, j0 = (0, P * c) if c < 4 else (c // 2 - 1, P * (c % 2))
+            nc.vector.tensor_tensor(
+                out=h_b[c // 2][:, 512 * (c % 2) : 512 * (c % 2 + 1)].rearrange("p (c i t) -> p c t i", i=4, t=4),
+                in0=acc[c][:].rearrange("p (t c i) -> p c t i", t=4, i=4),
+                in1=lim_t[piece][:, :, j0 : j0 + P].rearrange("p t (c i) -> p c t i", i=4),
+                op=ALU.min,
+            )
+
+        def quantize_h(k):
+            nc.vector.quantize_mx(out=h_q[k][:].bitcast(FP8X4), scales=h_s[k][:], in_=h_b[k][:])
+
+        def bounded_part(q, k):
+            bank = psum.tile([P, 512], F32, name="pa", tag="ab")
+            for cc in range(2):
+                js = slice(P * cc, P * (cc + 1))
+                nc.tensor.matmul_mx(
+                    out=bank[:, 256 * cc : 256 * (cc + 1)],
+                    lhsT=h_q[k][:, js].bitcast(FP8X4),
+                    lhsT_scale=h_s[k][:, js],
+                    rhs=w2_q[:, 512 * q : 512 * (q + 1)].bitcast(FP4X4),
+                    rhs_scale=w2_s[:, 256 * q : 256 * (q + 1)],
+                    start=True,
+                    stop=True,
+                )
+            nc.scalar.activation(out=parts[q][:, 512 * k : 512 * (k + 1)], in_=bank[:], func=ACT.Tanh)
+
+        def plain_part(q, k, copy):
+            bank = psum.tile([P, 512], F32, name="pb", tag="ab")
+            for cc in range(2):
+                js = slice(P * cc, P * (cc + 1))
+                nc.tensor.matmul_mx(
+                    out=bank[:, 256 * cc : 256 * (cc + 1)],
+                    lhsT=h_q[k][:, js].bitcast(FP8X4),
+                    lhsT_scale=h_s[k][:, js],
+                    rhs=w3_q[q][:].bitcast(FP8X4),
+                    rhs_scale=w3_s[q][:],
+                    start=True,
+                    stop=True,
+                )
+            copy(out=parts[q][:, 2048 + 512 * k : 2048 + 512 * (k + 1)], in_=bank[:])
+
+        w3_b = [
+            ring.tile([P, 2048], BF16, name="w3b%d" % g, tag="staged", bufs=3, align_bytes=64)
+            for g in range(GROUPS)
+        ]
+
+        def prepare_w3(q):
+            g, u = divmod(q, 2)
+            deal(nc.scalar.copy, w3_raw[g], w3_b[g], 2 * u, 2 * u + 2)
+            nc.vector.quantize_mx(
+                out=w3_q[q][:].bitcast(FP8X4), scales=w3_s[q][:], in_=w3_b[g][:, 1024 * u : 1024 * (u + 1)]
+            )
+
+        for k in range(PAIRS):
+            cap(2 * k)
+            if k > 0:
+                quantize_h(k - 1)
+                bounded_part(0, k - 1)
+            if k == 2:
+                prepare_w3(0)
+                plain_part(0, 0, nc.scalar.copy)
+            if k > 1:
+                plain_part(0, k - 1, nc.scalar.copy)
+            cap(2 * k + 1)
+        quantize_h(PAIRS - 1)
+        bounded_part(0, PAIRS - 1)
+        plain_part(0, PAIRS - 1, nc.vector.tensor_copy)
+
+        neg_open = keep.tile([P, 4 * GROUPS], F32, name="neg_open")
+        nc.vector.scalar_tensor_tensor(
+            out=neg_open[:], in0=slope_t[:], scalar=-1.0, in1=share_t[:], op0=ALU.mult, op1=ALU.mult
+        )
+        tops = keep.tile([P, 8 * GROUPS], F32, name="tops")
+        bias = keep.tile([P, 4 * GROUPS], F32, name="bias")
+        y = [
+            ring.tile([P, 4, M], F32, name="y%d" % g, tag="raw", bufs=3, align_bytes=64)
+            for g in range(GROUPS)
+        ]
+        looks, picks = {}, {}
+        last = 4 * GROUPS - 1
+
+        def spans(i):
+            return [(0, M // 2), (M // 2, M)] if i == last else [(0, M)]
+
+        def scores(i):
+            q, tt = divmod(i, 2)
+            e = ring.tile([P, S], F32, name="e", tag="e", bufs=3, align_bytes=64)
+            for half in range(2):
+                bank = psum.tile([P, 512], F32, name="pe", tag="e")
+                for cc in range(4):
+                    c = 4 * half + cc
+                    at = 256 * c + P * tt
+                    for part in range(2):
+                        nc.tensor.matmul(
+                            out=bank[:, P * cc : P * (cc + 1)],
+                            lhsT=parts[q][:, 2048 * part + at : 2048 * part + at + P],
+                            rhs=ident[:],
+                            start=(part == 0),
+                            stop=(part == 1),
+                            is_transpose=True,
+                        )
+                nc.vector.tensor_scalar(
+                    out=e[:, 512 * half : 512 * (half + 1)], in0=bank[:], scalar1=1.0, scalar2=None,
+                    op0=ALU.mult, op1=ALU.max, accum_out=tops[:, 2 * i + half : 2 * i + half + 1],
+                )
+            nc.vector.tensor_scalar(
+                out=bias[:, i : i + 1], in0=tops[:, 2 * i : 2 * i + 1], scalar1=tops[:, 2 * i + 1 : 2 * i + 2],
+                scalar2=neg_open[:, i : i + 1], op0=ALU.max, op1=ALU.mult,
+            )
+            looks[i] = ring.tile([P, M], F32, name="look", tag="look", bufs=3, align_bytes=64)
+            picks[i] = ring.tile([P, M], F32, name="pick", tag="pick", bufs=3, align_bytes=64)
+            for m0, m1 in spans(i):
+                nc.scalar.activation(
+                    out=looks[i][:, m0:m1], in_=e[:].indirect(pos1_t[:, m0 // 16 : m1 // 16]), func=ACT.Sigmoid,
+                    bias=bias[:, i : i + 1], scale=slope_t[:, i : i + 1],
+                )
+                nc.vector.tensor_copy(picks[i][:, m0:m1], e[:].indirect(pos2_t[:, m0 // 16 : m1 // 16]))
+
+        def finish(i):
+            g, t = divmod(i, 4)
+            opened = ring.tile([P, M], F32, name="opened", tag="opened", bufs=2, align_bytes=64)
+            for m0, m1 in spans(i):
+                nc.vector.scalar_tensor_tensor(
+                    out=opened[:, m0:m1], in0=looks[i][:, m0:m1], scalar=sgn_t[:, i : i + 1],
+                    in1=base_t[g][:, t, m0:m1], op0=ALU.mult, op1=ALU.add,
+                )
+                nc.vector.scalar_tensor_tensor(
+                    out=y[g][:, t, m0:m1], in0=picks[i][:, m0:m1], scalar=gain_t[:, i : i + 1],
+                    in1=opened[:, m0:m1], op0=ALU.mult, op1=ALU.min,
+                )
+            nc.sync.dma_start(
+                out=out_0[512 * g : 512 * (g + 1), :].rearrange("(p t) m -> p t m", t=4)[:, t, :],
+                in_=y[g][:, t, :],
+            )
+
+        def planes(g):
+            y_b = ring.tile([P, 2048], BF16, name="yb%d" % g, tag="staged", bufs=3, align_bytes=64)
+            y_q = keep.tile([P, M], U32, name="yq%d" % g, align_bytes=64)
+            y_s = keep.tile([P, M], U8, name="ys%d" % g, align_bytes=64)
+            for m0, m1 in spans(4 * g + 3):
+                copy = nc.vector.tensor_copy if m0 > 0 else nc.scalar.copy
+                copy(
+                    out=y_b[:, 4 * m0 : 4 * m1].rearrange("p (c i t) -> p c t i", i=4, t=4),
+                    in_=y[g][:, :, m0:m1].rearrange("p t (c i) -> p c t i", i=4),
+                )
+            for m0, m1 in spans(4 * g + 3):
+                nc.vector.quantize_mx(
+                    out=y_q[:, m0:m1].bitcast(FP8X4), scales=y_s[:, m0:m1], in_=y_b[:, 4 * m0 : 4 * m1]
+                )
+                nc.sync.dma_start(
+                    out=out_1[g].rearrange("p m t -> p (m t)").bitcast(I32)[:, m0:m1],
+                    in_=y_q[:, m0:m1].bitcast(I32),
+                )
+            for q in range(4):
+                nc.sync.dma_start(
+                    out=out_2[g, 4 * q : 4 * q + 4, :].bitcast(I32),
+                    in_=y_s[32 * q : 32 * q + 4, :].bitcast(I32),
+                )
+
+        for i in range(4 * GROUPS):
+            q, tt = divmod(i, 2)
+            scores(i)
+            if i > 0:
+                finish(i - 1)
+            if i == 4:
+                planes(0)
+            if q + 1 < 4:
+                if tt == 0:
+                    prepare_w3(q + 1)
+                for k in range(2 * tt, 2 * tt + 2):
+                    bounded_part(q + 1, k)
+                    plain_part(q + 1, k, nc.scalar.copy)
+        finish(4 * GROUPS - 1)
+        planes(GROUPS - 1)

@@ -44,12 +44,13 @@ def tile_list_pallet_shortage_scores_kernel(
         w2_s = keep.tile([P, N], U8, name="w2_s", align_bytes=64)
         v_s = keep.tile([P, S], U8, name="v_s", align_bytes=64)
         ident = keep.tile([P, P], F32, name="ident", align_bytes=64)
-        make_identity(nc, ident[:])
-        nc.vector.memset(tab_s[:].bitcast(I32), 0)
+        nc.vector.memset(tab_s[:, : T // 2].bitcast(I32), 0)
+        nc.gpsimd.memset(tab_s[:, T // 2 :].bitcast(I32), 0)
         nc.vector.memset(w2s_raw[:].bitcast(I32), 0)
+        make_identity(nc, ident[:])
 
         def load_tab(a):
-            t = ring.tile([P, T], I32, name="tab%d" % a, tag="big", bufs=4, align_bytes=64)
+            t = ring.tile([P, T], I32, name="tab%d" % a, tag="big", bufs=3, align_bytes=64)
             nc.sync.dma_start(out=t[:], in_=tab_words[a].rearrange("p t i -> p (t i)").bitcast(I32))
             return t
 
@@ -60,11 +61,14 @@ def tile_list_pallet_shortage_scores_kernel(
 
         def load_vec(src, name):
             t = keep.tile([P, 4 * GROUPS], F32, name=name)
-            nc.gpsimd.dma_start(
+            nc.sync.dma_start(
                 out=t[:].rearrange("p (g t) -> p g t", t=4),
                 in_=src.rearrange("(g p t) -> p g t", p=P, t=4),
             )
             return t
+
+        def load_scales(dst, src, rows, q):
+            nc.sync.dma_start(out=dst[32 * q : 32 * q + rows, :].bitcast(I32), in_=src.bitcast(I32))
 
         tab, w1_raw = [], []
         tab.append(load_tab(0))
@@ -72,31 +76,31 @@ def tile_list_pallet_shortage_scores_kernel(
         w1_raw.append(load_rows(w1[0:512, :], "w1r0", "raw", 3))
         nc.sync.dma_start(out=w2_raw[:].bitcast(I32), in_=w2_words[0].bitcast(I32))
         for q in range(4):
-            nc.sync.dma_start(
-                out=tab_s[32 * q : 32 * q + 4 * PASSES, :].bitcast(I32),
-                in_=tab_scales[:, 4 * q : 4 * q + 4, :].bitcast(I32),
-            )
+            load_scales(tab_s, tab_scales[:, 4 * q : 4 * q + 4, :], 4 * PASSES, q)
         tab.append(load_tab(1))
-        for q in range(4):
-            nc.gpsimd.dma_start(
-                out=w2s_raw[32 * q : 32 * q + 4, :].bitcast(I32),
-                in_=w2_scales[0, 4 * q : 4 * q + 4, :].bitcast(I32),
-            )
         w1_raw.append(load_rows(w1[512:1024, :], "w1r1", "raw", 3))
+        for q in range(4):
+            load_scales(w2s_raw, w2_scales[0, 4 * q : 4 * q + 4, :], 4, q)
         tab.append(load_tab(2))
         w1_raw.append(load_rows(w1[1024:1536, :], "w1r2", "raw", 3))
-        lim_t = [load_rows(lim[:, 0:512], "lim0", "lim0", 1)]
+        lim_all = keep.tile([P, 4 * S], F32, name="lim_all", align_bytes=64)
+
+        def load_lim(j0, j1):
+            piece = lim_all[:, 4 * j0 : 4 * j1].rearrange("p (t j) -> p t j", t=4)
+            nc.sync.dma_start(out=piece, in_=lim[:, j0:j1].rearrange("(p t) j -> p t j", t=4))
+            return piece
+
+        lim_t = [load_lim(0, 512), load_lim(512, 768)]
         w3_raw = [load_rows(w3[:, 0:512], "w3r0", "w3r", 2)]
-        lim_t.append(load_rows(lim[:, 512:768], "lim1", "lim1", 1))
-        lim_t.append(load_rows(lim[:, 768:1024], "lim2", "lim2", 1))
-        w3_raw.append(load_rows(w3[:, 512:1024], "w3r1", "w3r", 2))
-        nc.sync.dma_start(pos1_t[:], pos1)
-        nc.sync.dma_start(pos2_t[:], pos2)
+        lim_t.append(load_lim(768, 1024))
         slope_t = load_vec(slope, "slope_t")
         share_t = load_vec(share, "share_t")
+        nc.sync.dma_start(pos1_t[:], pos1)
+        nc.sync.dma_start(pos2_t[:], pos2)
+        base_t = [load_rows(base[0:512, :], "base0", "base", 2)]
         sgn_t = load_vec(sgn, "sgn_t")
         gain_t = load_vec(gain, "gain_t")
-        base_t = [load_rows(base[0:512, :], "base0", "base", 2)]
+        w3_raw.append(load_rows(w3[:, 512:1024], "w3r1", "w3r", 2))
         base_t.append(load_rows(base[512:1024, :], "base1", "base", 2))
 
         def deal(copy, raw, staged, t0, t1):
@@ -123,7 +127,7 @@ def tile_list_pallet_shortage_scores_kernel(
             w1_q = keep.tile([P, 512], U32, name="w1q%d" % a, align_bytes=64)
             w1_s = keep.tile([P, 512], U8, name="w1s%d" % a, align_bytes=64)
             nc.vector.quantize_mx(out=w1_q[:].bitcast(FP8X4), scales=w1_s[:], in_=staged[:])
-            if a == 0:
+            if a == 1:
                 nc.vector.tensor_copy(
                     out=w2_q[:].rearrange("p (g t m b) -> p g t m b", g=GROUPS, t=4, b=2),
                     in_=w2_raw[:].rearrange("p (g m t b) -> p g t m b", g=GROUPS, t=4, b=2),
@@ -154,10 +158,8 @@ def tile_list_pallet_shortage_scores_kernel(
         ]
         w3_q = [keep.tile([P, 256], U32, name="w3q%d" % q, align_bytes=64) for q in range(4)]
         w3_s = [keep.tile([P, 256], U8, name="w3s%d" % q, align_bytes=64) for q in range(4)]
-        parts = [
-            ring.tile([P, 4096], F32, name="parts%d" % q, tag="big", bufs=4, align_bytes=64)
-            for q in range(4)
-        ]
+        parts_even = ring.tile([P, 4096], F32, name="parts_even", tag="big", bufs=3, align_bytes=64)
+        parts = [parts_even, lim_all, parts_even, lim_all]
 
         def cap(c):
             piece, j0 = (0, P * c) if c < 4 else (c // 2 - 1, P * (c % 2))
@@ -184,7 +186,7 @@ def tile_list_pallet_shortage_scores_kernel(
                     start=True,
                     stop=True,
                 )
-            nc.scalar.activation(out=parts[q][:, 512 * k : 512 * (k + 1)], in_=bank[:], func=ACT.Tanh)
+            nc.scalar.activation(out=parts[q][:, 2048 + 512 * k : 2048 + 512 * (k + 1)], in_=bank[:], func=ACT.Tanh)
 
         def plain_part(q, k, copy):
             bank = psum.tile([P, 512], F32, name="pb", tag="ab")
@@ -199,38 +201,45 @@ def tile_list_pallet_shortage_scores_kernel(
                     start=True,
                     stop=True,
                 )
-            copy(out=parts[q][:, 2048 + 512 * k : 2048 + 512 * (k + 1)], in_=bank[:])
+            copy(out=parts[q][:, 512 * k : 512 * (k + 1)], in_=bank[:])
 
-        w3_b = [
-            ring.tile([P, 2048], BF16, name="w3b%d" % g, tag="staged", bufs=3, align_bytes=64)
-            for g in range(GROUPS)
-        ]
+        w3_first = keep.tile([P, 1024], BF16, name="w3_first", align_bytes=64)
+        w3_b = [w3_first, h_b[3], h_b[2], h_b[3]]
 
-        def prepare_w3(q):
+        def round_w3(q):
             g, u = divmod(q, 2)
-            deal(nc.scalar.copy, w3_raw[g], w3_b[g], 2 * u, 2 * u + 2)
-            nc.vector.quantize_mx(
-                out=w3_q[q][:].bitcast(FP8X4), scales=w3_s[q][:], in_=w3_b[g][:, 1024 * u : 1024 * (u + 1)]
+            copy = nc.vector.tensor_copy if q == 0 else nc.scalar.copy
+            copy(
+                out=w3_b[q][:].rearrange("p (t m j) -> p m j t", t=2, j=4),
+                in_=w3_raw[g][:].rearrange("p j (m t) -> p m j t", t=4)[:, :, :, 2 * u : 2 * u + 2],
             )
 
+        def quantize_w3(q):
+            nc.vector.quantize_mx(out=w3_q[q][:].bitcast(FP8X4), scales=w3_s[q][:], in_=w3_b[q][:])
+
+        def prepare_w3(q):
+            round_w3(q)
+            quantize_w3(q)
+
+        round_w3(0)
+        cap(0)
         for k in range(PAIRS):
-            cap(2 * k)
-            if k > 0:
-                quantize_h(k - 1)
-                bounded_part(0, k - 1)
-            if k == 2:
-                prepare_w3(0)
-                plain_part(0, 0, nc.scalar.copy)
-            if k > 1:
-                plain_part(0, k - 1, nc.scalar.copy)
             cap(2 * k + 1)
-        quantize_h(PAIRS - 1)
-        bounded_part(0, PAIRS - 1)
+            if k + 1 < PAIRS:
+                cap(2 * k + 2)
+            quantize_h(k)
+            bounded_part(0, k)
+            if k == PAIRS - 2:
+                quantize_w3(0)
+                for early in range(PAIRS - 1):
+                    plain_part(0, early, nc.scalar.copy)
         plain_part(0, PAIRS - 1, nc.vector.tensor_copy)
 
         neg_open = keep.tile([P, 4 * GROUPS], F32, name="neg_open")
-        nc.vector.scalar_tensor_tensor(
-            out=neg_open[:], in0=slope_t[:], scalar=-1.0, in1=share_t[:], op0=ALU.mult, op1=ALU.mult
+        open_t = keep.tile([P, 4 * GROUPS], F32, name="open_t")
+        nc.gpsimd.tensor_tensor(out=open_t[:], in0=slope_t[:], in1=share_t[:], op=ALU.mult)
+        nc.gpsimd.tensor_scalar(
+            out=neg_open[:], in0=open_t[:], scalar1=-1.0, scalar2=0.0, op0=ALU.mult, op1=ALU.add
         )
         tops = keep.tile([P, 8 * GROUPS], F32, name="tops")
         bias = keep.tile([P, 4 * GROUPS], F32, name="bias")
@@ -246,7 +255,7 @@ def tile_list_pallet_shortage_scores_kernel(
 
         def scores(i):
             q, tt = divmod(i, 2)
-            e = ring.tile([P, S], F32, name="e", tag="e", bufs=3, align_bytes=64)
+            e = ring.tile([P, S], F32, name="e", tag="e", bufs=4, align_bytes=64)
             for half in range(2):
                 bank = psum.tile([P, 512], F32, name="pe", tag="e")
                 for cc in range(4):
@@ -296,7 +305,7 @@ def tile_list_pallet_shortage_scores_kernel(
             )
 
         def planes(g):
-            y_b = ring.tile([P, 2048], BF16, name="yb%d" % g, tag="staged", bufs=3, align_bytes=64)
+            y_b = parts_even[:, 1024 * g : 1024 * (g + 1)].bitcast(BF16)
             y_q = keep.tile([P, M], U32, name="yq%d" % g, align_bytes=64)
             y_s = keep.tile([P, M], U8, name="ys%d" % g, align_bytes=64)
             for m0, m1 in spans(4 * g + 3):
@@ -324,7 +333,7 @@ def tile_list_pallet_shortage_scores_kernel(
             scores(i)
             if i > 0:
                 finish(i - 1)
-            if i == 4:
+            if i == 6:
                 planes(0)
             if q + 1 < 4:
                 if tt == 0:

@@ -44,8 +44,7 @@ def tile_list_pallet_shortage_scores_kernel(
         w2_s = keep.tile([P, N], U8, name="w2_s", align_bytes=64)
         v_s = keep.tile([P, S], U8, name="v_s", align_bytes=64)
         ident = keep.tile([P, P], F32, name="ident", align_bytes=64)
-        nc.vector.memset(tab_s[:, : T // 2].bitcast(I32), 0)
-        nc.gpsimd.memset(tab_s[:, T // 2 :].bitcast(I32), 0)
+        nc.vector.memset(tab_s[:].bitcast(I32), 0)
         nc.vector.memset(w2s_raw[:].bitcast(I32), 0)
         make_identity(nc, ident[:])
 
@@ -68,7 +67,7 @@ def tile_list_pallet_shortage_scores_kernel(
             return t
 
         def load_scales(dst, src, rows, q):
-            nc.sync.dma_start(out=dst[32 * q : 32 * q + rows, :].bitcast(I32), in_=src.bitcast(I32))
+            nc.gpsimd.dma_start(out=dst[32 * q : 32 * q + rows, :].bitcast(I32), in_=src.bitcast(I32))
 
         tab, w1_raw = [], []
         tab.append(load_tab(0))
@@ -159,7 +158,9 @@ def tile_list_pallet_shortage_scores_kernel(
         w3_q = [keep.tile([P, 256], U32, name="w3q%d" % q, align_bytes=64) for q in range(4)]
         w3_s = [keep.tile([P, 256], U8, name="w3s%d" % q, align_bytes=64) for q in range(4)]
         parts_even = ring.tile([P, 4096], F32, name="parts_even", tag="big", bufs=3, align_bytes=64)
-        parts = [parts_even, lim_all, parts_even, lim_all]
+        flat = "p j c -> p (j c)"
+        bounded = [parts_even[:, 2048:], lim_all[:, 2048:], w3_raw[0][:].rearrange(flat), w3_raw[1][:].rearrange(flat)]
+        plain = [parts_even[:, :2048], lim_all[:, :2048], parts_even[:, :2048], lim_all[:, :2048]]
 
         def cap(c):
             piece, j0 = (0, P * c) if c < 4 else (c // 2 - 1, P * (c % 2))
@@ -186,7 +187,7 @@ def tile_list_pallet_shortage_scores_kernel(
                     start=True,
                     stop=True,
                 )
-            nc.scalar.activation(out=parts[q][:, 2048 + 512 * k : 2048 + 512 * (k + 1)], in_=bank[:], func=ACT.Tanh)
+            nc.scalar.activation(out=bounded[q][:, 512 * k : 512 * (k + 1)], in_=bank[:], func=ACT.Tanh)
 
         def plain_part(q, k, copy):
             bank = psum.tile([P, 512], F32, name="pb", tag="ab")
@@ -201,7 +202,7 @@ def tile_list_pallet_shortage_scores_kernel(
                     start=True,
                     stop=True,
                 )
-            copy(out=parts[q][:, 512 * k : 512 * (k + 1)], in_=bank[:])
+            copy(out=plain[q][:, 512 * k : 512 * (k + 1)], in_=bank[:])
 
         w3_first = keep.tile([P, 1024], BF16, name="w3_first", align_bytes=64)
         w3_b = [w3_first, h_b[3], h_b[2], h_b[3]]
@@ -261,10 +262,10 @@ def tile_list_pallet_shortage_scores_kernel(
                 for cc in range(4):
                     c = 4 * half + cc
                     at = 256 * c + P * tt
-                    for part in range(2):
+                    for part, source in enumerate((plain[q], bounded[q])):
                         nc.tensor.matmul(
                             out=bank[:, P * cc : P * (cc + 1)],
-                            lhsT=parts[q][:, 2048 * part + at : 2048 * part + at + P],
+                            lhsT=source[:, at : at + P],
                             rhs=ident[:],
                             start=(part == 0),
                             stop=(part == 1),

@@ -47,6 +47,8 @@ def tile_list_pallet_shortage_scores_kernel(
         nc.vector.memset(tab_s[:].bitcast(I32), 0)
         nc.vector.memset(w2s_raw[:].bitcast(I32), 0)
         make_identity(nc, ident[:])
+        table_warm = keep.tile([P, 1], F32, name="table_warm")
+        nc.scalar.activation(out=table_warm[:], in_=ident[:, 0:1], func=ACT.Sigmoid)
 
         def load_tab(a):
             t = ring.tile([P, T], I32, name="tab%d" % a, tag="big", bufs=3, align_bytes=64)

from contextlib import ExitStack

import concourse.mybir as mybir
from concourse.masks import make_identity

K, T, S, H, N, M = 1536, 4096, 1024, 512, 1024, 512
FLOPS = 2 * K * H * S + 2 * 2 * H * N * S

F32 = mybir.dt.float32
BF16 = mybir.dt.bfloat16
I32 = mybir.dt.int32
U32 = mybir.dt.uint32
U16 = mybir.dt.uint16
U8 = mybir.dt.uint8
FP8X4 = mybir.dt.float8_e4m3fn_x4
FP4X4 = mybir.dt.float4_e2m1fn_x4
ALU = mybir.AluOpType
ACT = mybir.ActivationFunctionType

P = 128
PASSES = K // 512
CHUNKS = S // P
PAIRS = CHUNKS // 2
GROUPS = N // 512


def tile_list_pallet_shortage_scores_kernel(
    tc, tab_words, tab_scales, offs, pos1, pos2, w1, lim, w2_words, w2_scales, w3,
    slope, share, sgn, base, gain, out_0, out_1, out_2,
):
    nc = tc.nc
    with ExitStack() as ctx:
        keep = ctx.enter_context(tc.tile_pool(name="keep", bufs=1))
        ring = ctx.enter_context(tc.tile_pool(name="ring", bufs=2))
        psum = ctx.enter_context(tc.psum_pool(name="psum", bufs=4))

        offs_t = keep.tile([P, S // 16], U16, name="offs_t")
        pos1_t = keep.tile([P, M // 16], U16, name="pos1_t")
        pos2_t = keep.tile([P, M // 16], U16, name="pos2_t")
        tab_s = keep.tile([P, T], U8, name="tab_s", align_bytes=64)
        w2_raw = keep.tile([P, 2 * N], U8, name="w2_raw", align_bytes=64)
        w2s_raw = keep.tile([P, N], U8, name="w2s_raw", align_bytes=64)
        w2_q = keep.tile([P, 2 * N], U8, name="w2_q", align_bytes=64)
        w2_s = keep.tile([P, N], U8, name="w2_s", align_bytes=64)
        v_s = keep.tile([P, S], U8, name="v_s", align_bytes=64)
        ident = keep.tile([P, P], F32, name="ident", align_bytes=64)
        nc.vector.memset(tab_s[:].bitcast(I32), 0)
        nc.vector.memset(w2s_raw[:].bitcast(I32), 0)
        make_identity(nc, ident[:])
        table_warm = keep.tile([P, 1], F32, name="table_warm")
        nc.scalar.activation(out=table_warm[:], in_=ident[:, 0:1], func=ACT.Sigmoid)

        def load_tab(a):
            t = ring.tile([P, T], I32, name="tab%d" % a, tag="big", bufs=3, align_bytes=64)
            nc.sync.dma_start(out=t[:], in_=tab_words[a].rearrange("p t i -> p (t i)").bitcast(I32))
            return t

        def load_rows(src, name, tag, bufs):
            t = ring.tile([P, 4, src.shape[1]], F32, name=name, tag=tag, bufs=bufs, align_bytes=64)
            nc.sync.dma_start(out=t[:], in_=src.rearrange("(p j) c -> p j c", j=4))
            return t

        def load_vec(src, name):
            t = keep.tile([P, 4 * GROUPS], F32, name=name)
            nc.sync.dma_start(
                out=t[:].rearrange("p (g t) -> p g t", t=4),
                in_=src.rearrange("(g p t) -> p g t", p=P, t=4),
            )
            return t

        def load_scales(dst, src, rows, q):
            nc.gpsimd.dma_start(out=dst[32 * q : 32 * q + rows, :].bitcast(I32), in_=src.bitcast(I32))

        tab, w1_raw = [], []
        tab.append(load_tab(0))
        nc.sync.dma_start(offs_t[:], offs)
        w1_raw.append(load_rows(w1[0:512, :], "w1r0", "raw", 3))
        nc.sync.dma_start(out=w2_raw[:].bitcast(I32), in_=w2_words[0].bitcast(I32))
        for q in range(4):
            load_scales(tab_s, tab_scales[:, 4 * q : 4 * q + 4, :], 4 * PASSES, q)
        tab.append(load_tab(1))
        w1_raw.append(load_rows(w1[512:1024, :], "w1r1", "raw", 3))
        for q in range(4):
            load_scales(w2s_raw, w2_scales[0, 4 * q : 4 * q + 4, :], 4, q)
        tab.append(load_tab(2))
        w1_raw.append(load_rows(w1[1024:1536, :], "w1r2", "raw", 3))
        lim_all = keep.tile([P, 4 * S], F32, name="lim_all", align_bytes=64)

        def load_lim(j0, j1):
            piece = lim_all[:, 4 * j0 : 4 * j1].rearrange("p (t j) -> p t j", t=4)
            nc.sync.dma_start(out=piece, in_=lim[:, j0:j1].rearrange("(p t) j -> p t j", t=4))
            return piece

        lim_t = [load_lim(0, 512), load_lim(512, 768)]
        w3_raw = [load_rows(w3[:, 0:512], "w3r0", "w3r", 2)]
        lim_t.append(load_lim(768, 1024))
        slope_t = load_vec(slope, "slope_t")
        share_t = load_vec(share, "share_t")
        nc.sync.dma_start(pos1_t[:], pos1)
        nc.sync.dma_start(pos2_t[:], pos2)
        base_t = [load_rows(base[0:512, :], "base0", "base", 2)]
        sgn_t = load_vec(sgn, "sgn_t")
        gain_t = load_vec(gain, "gain_t")
        w3_raw.append(load_rows(w3[:, 512:1024], "w3r1", "w3r", 2))
        base_t.append(load_rows(base[512:1024, :], "base1", "base", 2))

        def deal(copy, raw, staged, t0, t1):
            copy(
                out=staged[:].rearrange("p (t m j) -> p m j t", t=4, j=4)[:, :, :, t0:t1],
                in_=raw[:].rearrange("p j (m t) -> p m j t", t=4)[:, :, :, t0:t1],
            )

        acc = [
            psum.tile([P, 512], F32, name="acc%d" % c, tag="ab" if c < 4 else "e")
            for c in range(CHUNKS)
        ]
        for a in range(PASSES):
            v_w = keep.tile([P, S], U32, name="v_w%d" % a, align_bytes=64)
            nc.vector.tensor_copy(v_w[:], tab[a][:].bitcast(U32).indirect(offs_t[:]))
            if a == 0:
                nc.vector.tensor_copy(v_s[:], tab_s[:].indirect(offs_t[:]))
            staged = ring.tile([P, 2048], BF16, name="w1b%d" % a, tag="staged", bufs=3, align_bytes=64)
            if a == PASSES - 1:
                deal(nc.scalar.copy, w1_raw[a], staged, 0, 1)
                deal(nc.vector.tensor_copy, w1_raw[a], staged, 1, 4)
            else:
                deal(nc.scalar.copy, w1_raw[a], staged, 0, 4)
            w1_q = keep.tile([P, 512], U32, name="w1q%d" % a, align_bytes=64)
            w1_s = keep.tile([P, 512], U8, name="w1s%d" % a, align_bytes=64)
            nc.vector.quantize_mx(out=w1_q[:].bitcast(FP8X4), scales=w1_s[:], in_=staged[:])
            if a == 1:
                nc.vector.tensor_copy(
                    out=w2_q[:].rearrange("p (g t m b) -> p g t m b", g=GROUPS, t=4, b=2),
                    in_=w2_raw[:].rearrange("p (g m t b) -> p g t m b", g=GROUPS, t=4, b=2),
                )
                nc.vector.tensor_copy(
                    out=w2_s[:].rearrange("p (g t m) -> p g t m", g=GROUPS, t=4),
                    in_=w2s_raw[:].rearrange("p (g m t) -> p g t m", g=GROUPS, t=4),
                )
            for c in range(CHUNKS):
                cols = slice(P * c, P * (c + 1))
                for t in range(4):
                    rows = slice(P * t, P * (t + 1))
                    nc.tensor.matmul_mx(
                        out=acc[c][:, rows],
                        lhsT=w1_q[:, rows].bitcast(FP8X4),
                        lhsT_scale=w1_s[:, rows],
                        rhs=v_w[:, cols].bitcast(FP8X4),
                        rhs_scale=v_s[4 * a : P, cols],
                        start=(a == 0 and t == 0),
                        stop=(a == PASSES - 1 and t == 3),
                    )

        h_q = [keep.tile([P, 256], U32, name="hq%d" % k, align_bytes=64) for k in range(PAIRS)]
        h_s = [keep.tile([P, 256], U8, name="hs%d" % k, align_bytes=64) for k in range(PAIRS)]
        h_b = [
            ring.tile([P, 1024], BF16, name="hb%d" % k, tag="hb", bufs=4, align_bytes=64)
            for k in range(PAIRS)
        ]
        w3_q = [keep.tile([P, 256], U32, name="w3q%d" % q, align_bytes=64) for q in range(4)]
        w3_s = [keep.tile([P, 256], U8, name="w3s%d" % q, align_bytes=64) for q in range(4)]
        parts_even = ring.tile([P, 4096], F32, name="parts_even", tag="big", bufs=3, align_bytes=64)
        flat = "p j c -> p (j c)"
        bounded = [parts_even[:, 2048:], lim_all[:, 2048:], w3_raw[0][:].rearrange(flat), w3_raw[1][:].rearrange(flat)]
        plain = [parts_even[:, :2048], lim_all[:, :2048], parts_even[:, :2048], lim_all[:, :2048]]

        def cap(c):
            piece, j0 = (0, P * c) if c < 4 else (c // 2 - 1, P * (c % 2))
            nc.vector.tensor_tensor(
                out=h_b[c // 2][:, 512 * (c % 2) : 512 * (c % 2 + 1)].rearrange("p (c i t) -> p c t i", i=4, t=4),
                in0=acc[c][:].rearrange("p (t c i) -> p c t i", t=4, i=4),
                in1=lim_t[piece][:, :, j0 : j0 + P].rearrange("p t (c i) -> p c t i", i=4),
                op=ALU.min,
            )

        def quantize_h(k):
            nc.vector.quantize_mx(out=h_q[k][:].bitcast(FP8X4), scales=h_s[k][:], in_=h_b[k][:])

        def bounded_part(q, k):
            bank = psum.tile([P, 512], F32, name="pa", tag="ab")
            for cc in range(2):
                js = slice(P * cc, P * (cc + 1))
                nc.tensor.matmul_mx(
                    out=bank[:, 256 * cc : 256 * (cc + 1)],
                    lhsT=h_q[k][:, js].bitcast(FP8X4),
                    lhsT_scale=h_s[k][:, js],
                    rhs=w2_q[:, 512 * q : 512 * (q + 1)].bitcast(FP4X4),
                    rhs_scale=w2_s[:, 256 * q : 256 * (q + 1)],
                    start=True,
                    stop=True,
                )
            nc.scalar.activation(out=bounded[q][:, 512 * k : 512 * (k + 1)], in_=bank[:], func=ACT.Tanh)

        def plain_part(q, k, copy):
            bank = psum.tile([P, 512], F32, name="pb", tag="ab")
            for cc in range(2):
                js = slice(P * cc, P * (cc + 1))
                nc.tensor.matmul_mx(
                    out=bank[:, 256 * cc : 256 * (cc + 1)],
                    lhsT=h_q[k][:, js].bitcast(FP8X4),
                    lhsT_scale=h_s[k][:, js],
                    rhs=w3_q[q][:].bitcast(FP8X4),
                    rhs_scale=w3_s[q][:],
                    start=True,
                    stop=True,
                )
            copy(out=plain[q][:, 512 * k : 512 * (k + 1)], in_=bank[:])

        w3_first = keep.tile([P, 1024], BF16, name="w3_first", align_bytes=64)
        w3_b = [w3_first, h_b[3], h_b[2], h_b[3]]

        def round_w3(q):
            g, u = divmod(q, 2)
            copy = nc.vector.tensor_copy if q == 0 else nc.scalar.copy
            copy(
                out=w3_b[q][:].rearrange("p (t m j) -> p m j t", t=2, j=4),
                in_=w3_raw[g][:].rearrange("p j (m t) -> p m j t", t=4)[:, :, :, 2 * u : 2 * u + 2],
            )

        def quantize_w3(q):
            nc.vector.quantize_mx(out=w3_q[q][:].bitcast(FP8X4), scales=w3_s[q][:], in_=w3_b[q][:])

        def prepare_w3(q):
            round_w3(q)
            quantize_w3(q)

        round_w3(0)
        cap(0)
        for k in range(PAIRS):
            cap(2 * k + 1)
            if k + 1 < PAIRS:
                cap(2 * k + 2)
            quantize_h(k)
            bounded_part(0, k)
            if k == PAIRS - 2:
                quantize_w3(0)
                for early in range(PAIRS - 1):
                    plain_part(0, early, nc.scalar.copy)
        plain_part(0, PAIRS - 1, nc.vector.tensor_copy)

        neg_open = keep.tile([P, 4 * GROUPS], F32, name="neg_open")
        open_t = keep.tile([P, 4 * GROUPS], F32, name="open_t")
        nc.gpsimd.tensor_tensor(out=open_t[:], in0=slope_t[:], in1=share_t[:], op=ALU.mult)
        nc.gpsimd.tensor_scalar(
            out=neg_open[:], in0=open_t[:], scalar1=-1.0, scalar2=0.0, op0=ALU.mult, op1=ALU.add
        )
        tops = keep.tile([P, 8 * GROUPS], F32, name="tops")
        bias = keep.tile([P, 4 * GROUPS], F32, name="bias")
        y = [
            ring.tile([P, 4, M], F32, name="y%d" % g, tag="raw", bufs=3, align_bytes=64)
            for g in range(GROUPS)
        ]
        looks, picks = {}, {}
        last = 4 * GROUPS - 1

        def spans(i):
            return [(0, M // 2), (M // 2, M)] if i == last else [(0, M)]

        def scores(i):
            q, tt = divmod(i, 2)
            e = ring.tile([P, S], F32, name="e", tag="e", bufs=4, align_bytes=64)
            for half in range(2):
                bank = psum.tile([P, 512], F32, name="pe", tag="e")
                for cc in range(4):
                    c = 4 * half + cc
                    at = 256 * c + P * tt
                    for part, source in enumerate((plain[q], bounded[q])):
                        nc.tensor.matmul(
                            out=bank[:, P * cc : P * (cc + 1)],
                            lhsT=source[:, at : at + P],
                            rhs=ident[:],
                            start=(part == 0),
                            stop=(part == 1),
                            is_transpose=True,
                        )
                nc.vector.tensor_scalar(
                    out=e[:, 512 * half : 512 * (half + 1)], in0=bank[:], scalar1=1.0, scalar2=None,
                    op0=ALU.mult, op1=ALU.max, accum_out=tops[:, 2 * i + half : 2 * i + half + 1],
                )
            nc.vector.tensor_scalar(
                out=bias[:, i : i + 1], in0=tops[:, 2 * i : 2 * i + 1], scalar1=tops[:, 2 * i + 1 : 2 * i + 2],
                scalar2=neg_open[:, i : i + 1], op0=ALU.max, op1=ALU.mult,
            )
            looks[i] = ring.tile([P, M], F32, name="look", tag="look", bufs=3, align_bytes=64)
            picks[i] = ring.tile([P, M], F32, name="pick", tag="pick", bufs=3, align_bytes=64)
            for m0, m1 in spans(i):
                nc.scalar.activation(
                    out=looks[i][:, m0:m1], in_=e[:].indirect(pos1_t[:, m0 // 16 : m1 // 16]), func=ACT.Sigmoid,
                    bias=bias[:, i : i + 1], scale=slope_t[:, i : i + 1],
                )
                nc.vector.tensor_copy(picks[i][:, m0:m1], e[:].indirect(pos2_t[:, m0 // 16 : m1 // 16]))

        def finish(i):
            g, t = divmod(i, 4)
            opened = ring.tile([P, M], F32, name="opened", tag="opened", bufs=2, align_bytes=64)
            for m0, m1 in spans(i):
                nc.vector.scalar_tensor_tensor(
                    out=opened[:, m0:m1], in0=looks[i][:, m0:m1], scalar=sgn_t[:, i : i + 1],
                    in1=base_t[g][:, t, m0:m1], op0=ALU.mult, op1=ALU.add,
                )
                nc.vector.scalar_tensor_tensor(
                    out=y[g][:, t, m0:m1], in0=picks[i][:, m0:m1], scalar=gain_t[:, i : i + 1],
                    in1=opened[:, m0:m1], op0=ALU.mult, op1=ALU.min,
                )
            nc.sync.dma_start(
                out=out_0[512 * g : 512 * (g + 1), :].rearrange("(p t) m -> p t m", t=4)[:, t, :],
                in_=y[g][:, t, :],
            )

        def planes(g):
            y_b = parts_even[:, 1024 * g : 1024 * (g + 1)].bitcast(BF16)
            y_q = keep.tile([P, M], U32, name="yq%d" % g, align_bytes=64)
            y_s = keep.tile([P, M], U8, name="ys%d" % g, align_bytes=64)
            for m0, m1 in spans(4 * g + 3):
                copy = nc.vector.tensor_copy if m0 > 0 else nc.scalar.copy
                copy(
                    out=y_b[:, 4 * m0 : 4 * m1].rearrange("p (c i t) -> p c t i", i=4, t=4),
                    in_=y[g][:, :, m0:m1].rearrange("p t (c i) -> p c t i", i=4),
                )
            for m0, m1 in spans(4 * g + 3):
                nc.vector.quantize_mx(
                    out=y_q[:, m0:m1].bitcast(FP8X4), scales=y_s[:, m0:m1], in_=y_b[:, 4 * m0 : 4 * m1]
                )
                nc.sync.dma_start(
                    out=out_1[g].rearrange("p m t -> p (m t)").bitcast(I32)[:, m0:m1],
                    in_=y_q[:, m0:m1].bitcast(I32),
                )
            for q in range(4):
                nc.sync.dma_start(
                    out=out_2[g, 4 * q : 4 * q + 4, :].bitcast(I32),
                    in_=y_s[32 * q : 32 * q + 4, :].bitcast(I32),
                )

        for i in range(4 * GROUPS):
            q, tt = divmod(i, 2)
            scores(i)
            if i > 0:
                finish(i - 1)
            if i == 6:
                planes(0)
            if q + 1 < 4:
                if tt == 0:
                    prepare_w3(q + 1)
                for k in range(2 * tt, 2 * tt + 2):
                    bounded_part(q + 1, k)
                    plain_part(q + 1, k, nc.scalar.copy)
        finish(4 * GROUPS - 1)
        planes(GROUPS - 1)
